import numpy as np, ml_dtypes
CORES = [1,5,17,21,33,37,49,53]
N = 8
BF = ml_dtypes.bfloat16
def gentries(a):
    return np.ascontiguousarray(a.reshape(8, 16, -1).transpose(0, 2, 1)).reshape(8, -1)
def gtable(e):
    e = np.asarray(e); return np.ascontiguousarray(e.reshape(8, -1, 16).transpose(0, 2, 1)).reshape(128, -1).astype(np.int32)
R, A, LV, Q = 1024, 2, 1, 128
def level(kids, h):
    return kids[h // LV].reshape(8, LV, R, A)[:, h % LV]
def sizes(kids, runs):
    s = [runs[0].astype(np.int64)]
    for h in range(N * LV):
        s.append(np.sum(s[-1][np.arange(8)[:, None, None], level(kids, h)], axis=-1))
    return s
def parts(kids, s, h, n):
    g = np.arange(8)[:, None]; c = level(kids, h)[g, n]
    e = np.add.accumulate(s[h][g[:, :, None], c], axis=-1)
    return c, np.concatenate([np.zeros_like(e[..., :1]), e[..., :-1]], axis=-1)
def put(d, tops, offs):
    d["top"] = np.stack([gtable(v) for v in tops]); d["off"] = np.stack([gtable(v) for v in offs]); return d
def ask(d, tops, u):
    z = sizes(d["kids"], d["runs"])[-1][np.arange(8)[None, :, None], tops]
    return put(d, tops, np.minimum((u * z).astype(np.int64), z - 1))
def setup_inputs(rng):
    d = {"kids": rng.integers(0, R, (N, 8, LV * A * R)).astype(np.int32), "letter": rng.integers(0, 1 << 24, (N, 8, R)).astype(np.int32), "runs": rng.integers(1, 16, (N, 8, R)).astype(np.int32)}
    return ask(d, rng.integers(0, R, (N, 8, Q)), rng.random((N, 8, Q)))
def setup_inputs_edges(rng):
    d = setup_inputs(rng); k = d["kids"]; d["kids"] = np.where(rng.random(k.shape) < 0.25, rng.choice(np.array([0, R - 1]), k.shape), k).astype(np.int32)
    s = sizes(d["kids"], d["runs"]); tops = rng.integers(0, R, (N, 8, Q)); tops[:, :, 0] = 0; tops[:, :, 1] = R - 1; offs = np.zeros((N, 8, Q), np.int64)
    for r in range(N):
        n = tops[r]; low = rng.integers(0, N * LV + 1, (8, Q)); last = rng.integers(0, 2, (8, Q))
        for h in range(N * LV - 1, -1, -1):
            b = np.where(h < low, last * (A - 1), rng.integers(0, A, (8, Q)))[..., None]
            c, w = parts(d["kids"], s, h, n)
            offs[r] += np.take_along_axis(w, b, -1)[..., 0]; n = np.take_along_axis(c, b, -1)[..., 0]
        offs[r] += last * (s[0][np.arange(8)[:, None], n] - 1)
    return put(d, tops, offs)
def setup_inputs_runs(rng):
    d = setup_inputs(rng); d["runs"] = rng.choice(np.array([1, 15]), (N, 8, R)).astype(np.int32); a, b = rng.permutation(8)[:2]
    d["runs"][0, a] = 15; d["runs"][0, b] = 1
    u = rng.random((N, 8, Q)); m = rng.integers(0, 4, u.shape); u = np.where(m == 0, 0.0, np.where(m == 1, 1.0, u))
    return ask(d, rng.integers(0, R, (N, 8, Q)), u)
def setup_inputs_one(rng):
    d = setup_inputs(rng); k = d["kids"].reshape(N, 8, LV * R, A); t = rng.random((N, 8, LV * R, 1)) < 0.5
    d["kids"] = np.where(t, k[..., :1], k).reshape(N, 8, LV * A * R).astype(np.int32)
    tops = np.repeat(rng.integers(0, R, (N, 8, 1)), Q, axis=2); z = sizes(d["kids"], d["runs"])[-1][np.arange(8)[None, :, None], tops]
    start = (rng.random((N, 8, 1)) * z[:, :, :1]).astype(np.int64)
    offs = (start + np.arange(Q)[None, None, :]) % z; q = rng.integers(0, N)
    offs[q] = np.minimum((rng.random((8, 1)) * z[q]).astype(np.int64), z[q] - 1)
    return put(d, tops, offs)
def setup_inputs_spread(rng):
    d = setup_inputs(rng)
    d["kids"] = np.minimum((R * rng.random((N, 8, LV * A * R)) ** 4).astype(np.int32), R - 1)
    d["letter"] = np.minimum(np.exp2(24 * rng.random((N, 8, R))).astype(np.int32), (1 << 24) - 1)
    d["runs"] = np.minimum(1 + (15 * rng.random((N, 8, R)) ** 3).astype(np.int32), 15).astype(np.int32)
    return ask(d, np.minimum((R * rng.random((N, 8, Q)) ** 3).astype(np.int64), R - 1), rng.random((N, 8, Q)) ** 2)
def check_inputs(d):
    bad = []
    for k, lo, hi in (("kids", 0, R - 1), ("letter", 0, (1 << 24) - 1), ("runs", 1, 15), ("top", 0, R - 1)):
        if d[k].min() < lo or d[k].max() > hi: bad.append(k)
    if bad: return bad
    z = sizes(d["kids"], d["runs"])[-1]
    for r in range(N):
        o = gentries(d["off"][r]); n = gentries(d["top"][r])
        if (o < 0).any() or (o >= z[np.arange(8)[:, None], n]).any(): return ["off"]
    return []
def reference(kids, letter, runs, top, off):
    s = sizes(kids, runs); y = np.zeros((N, 8, Q), np.float32)
    for r in range(N):
        n = gentries(top[r]).astype(np.int64); o = gentries(off[r]).astype(np.int64)
        for h in range(N * LV - 1, -1, -1):
            c, w = parts(kids, s, h, n)
            b = np.sum(o[..., None] >= w[..., 1:], axis=-1)[..., None]
            o = o - np.take_along_axis(w, b, -1)[..., 0]; n = np.take_along_axis(c, b, -1)[..., 0]
        y[r] = letter[0][np.arange(8)[:, None], n]
    return {"y": y}

from concourse.bass import DstId, RemoteDMATransfer
from concourse.mybir import AluOpType, ActivationFunctionType

N = 8
TOP = 5
ND = 72

SCRATCH = {
    "sendK": ("dram", [8, 128, 16], "int32"), "pk0": ("dram", [8, 128, 32], "int32"),
    "sendQ": ("dram", [8, 128, 2], "int32"), "landK": ("dram", [8, 128, 16], "int32"),
    "land0": ("dram", [128, 32], "int32"), "landQ": ("dram", [8, 128, 2], "int32"),
    "outD": ("dram", [8, 128, 1], "float32"), "landY": ("dram", [8, 128, 1], "float32"),
}
for _d, _bufs in (
    ("float32", dict(X=4104, Zf=96, Zt=96, Zl=64, WW=896, GL=256, CL=768, CO=640, CF=128, RUf=128, J16=128, J8=128, J128=128,
                     PF=8, PA=32, LF=384, MK=8, RF=128, GE=384, GO=128, tb=160, GF=128, B=64)),
    ("int32", dict(Z=96, Zi=96, Za=96, CT=128, RU=128, PI=8, PB=8, topP=8, offP=8, ti=64, YU=16, RM=8)),
    ("uint16", dict(cls=96, col=96, OC=8, e1=24, tu=64, ix=64)),
    ("bfloat16", dict(M=2048, CW=128, RB=48, GN=512)),
    ("float16", dict(G=2048, LH=1024, RS=208, GD=768, O4=24, TT=64)),
):
    for _n, _w in _bufs.items():
        SCRATCH[_n] = ("sbuf", [128, _w], _d)
for _n in ("pW", "pV", "pC0", "pC1", "pL", "pT", "pD0", "pD1"):
    SCRATCH[_n] = ("psum", [128, 512], "float32")
SEMAPHORES = ["sv", "sa", "sp", "sg", "ls", "arrQ", "arrY"] + ["arrK%d" % h for h in range(N)] + ["d%d" % k for k in range(ND)]

ORDER = [1, 4, 2, 0, 3, 5, 11, 13, 14, 6, 7, 12, 10, 8, 9, 16, 35, 36, 37, 17, 38, 18, 39, 45, 40, 43, 44, 42, 15, 23, 25, 27, 21, 24, 19, 34, 33, 20, 22, 31, 32, 29, 26, 28, 30, 41, 53, 54, 50, 47, 51, 52, 48, 55, 73, 63, 49, 62, 56, 58, 46, 59, 64, 67, 57, 70, 65, 66, 74, 68, 69, 112, 75, 76, 81, 71, 72, 82, 95, 86, 83, 60, 98, 87, 88, 77, 78, 80, 79, 84, 85, 61, 89, 102, 101, 103, 106, 91, 92, 113, 90, 93, 99, 104, 105, 135, 94, 136, 107, 108, 137, 138, 114, 100, 122, 109, 123, 131, 128, 110, 111, 124, 117, 141, 142, 118, 127, 126, 132, 133, 129, 130, 147, 125, 146, 134, 148, 152, 162, 163, 164, 139, 165, 149, 158, 150, 159, 153, 151, 156, 167, 168, 160, 157, 115, 174, 175, 176, 177, 154, 140, 171, 172, 145, 116, 166, 185, 173, 182, 190, 178, 179, 180, 181, 183, 120, 121, 143, 97, 96, 161, 144, 155, 169, 170, 119, 184, 186, 187, 188, 189, 191, 192, 193, 194, 195, 196, 197, 200, 198, 199, 201, 202, 204, 203, 206, 220, 205, 207, 211, 212, 208, 210, 209, 215, 213, 214, 228, 216, 217, 219, 218, 223, 225, 229, 221, 222, 230, 231, 224, 227, 226, 233, 232, 234, 235, 236, 237]
QSEM = {"v": "sv", "a": "sa", "p": "sp", "g": "sg"}


def make_plan():
    ops, lastw, readers, bank = [], {}, {}, {}

    def op(q, fn, r=(), w=(), ext=(), dma=False, sem=None):
        deps, after = set(), set()
        for k in list(r) + list(w):
            if k.startswith("P:"):
                b = bank.setdefault(k, {})
                deps.update(i for qq, i in b.items() if qq != q)
                after.update(i for qq, i in b.items() if qq == q)
                b[q] = len(ops)
        r = [k for k in r if not k.startswith("P:")]
        w = [k for k in w if not k.startswith("P:")]
        for k in r:
            deps.update(lastw.get(k, []))
        for k in w:
            k0 = k.rstrip("+")
            if k0 == k:
                deps.update(lastw.get(k0, []))
            deps.update(readers.get(k0, []))
        for k in r:
            readers.setdefault(k, []).append(len(ops))
        for k in w:
            k0 = k.rstrip("+")
            if k0 == k:
                lastw[k0] = [len(ops)]
                readers[k0] = []
            else:
                lastw.setdefault(k0, []).append(len(ops))
        ops.append({"q": q, "fn": fn, "deps": sorted(deps), "after": sorted(after), "ext": list(ext), "dma": dma, "sem": sem})

    return ops, op


def emit(ops, order, queues, T):
    used = set(i for o in ops for i in o["deps"])
    count, nd, known, mark = {}, 0, {q: {} for q in queues}, {}
    place = {i: k for k, i in enumerate(order)}
    for i in order:
        o = ops[i]
        q, kn = o["q"], known[o["q"]]
        need = {}
        for s, v in o["ext"]:
            if kn.get(s, 0) < v:
                need[s] = max(need.get(s, 0), v)
        for d in sorted(o["deps"], key=place.get, reverse=True):
            s, v, clock = mark[d]
            if kn.get(s, 0) < v:
                need[s] = max(need.get(s, 0), v)
                for s2, v2 in clock.items():
                    if s2 not in need or need[s2] < v2:
                        kn[s2] = max(kn.get(s2, 0), v2)
        for s, v in need.items():
            queues[q].wait_ge(T.sem[s], v)
            kn[s] = max(kn.get(s, 0), v)
        ins = o["fn"]()
        if o["dma"]:
            if o["sem"] is not None:
                ins.then_inc(T.sem[o["sem"]], 16)
            else:
                s = "d%d" % nd
                nd += 1
                ins.then_inc(T.sem[s], 16)
                mark[i] = (s, 16, dict(kn))
                if i not in used:
                    queues[q].wait_ge(T.sem[s], 16)
        elif i in used:
            s = QSEM[q]
            count[s] = count.get(s, 0) + 1
            ins.then_inc(T.sem[s], 1)
            mark[i] = (s, count[s], dict(kn))


def rank_program(g, core, T, topo):
    me = T.rank_of(core)
    if me is None:
        return
    A, F = AluOpType, ActivationFunctionType
    V, S, P, Y = g.vector, g.scalar, g.tensor, g.sync
    ops, op = make_plan()
    peers = [r for r in range(N) if r != me]

    eng, taken = {}, []
    for r in sorted(peers, key=lambda r: len(topo.engines(core, T.cores[r]))):
        free = [e for e in topo.engines(core, T.cores[r]) if e not in taken]
        eng[r] = free[0]
        taken.append(free[0])
    sent = [0]

    def spread(src, dst, sem):
        ts = []
        for r in peers:
            rid, pid, _ = topo.addr(T.cores[r])
            ts.append(RemoteDMATransfer(dst_ids=[DstId(rid=rid, pnc=pid)], dma_engine_mask=1 << eng[r],
                                        remote_sem=T.sem[sem], src=src(r), dst=dst))
        sent[0] += len(ts)
        return g.remote_dma_fused(ts, local_sem=T.sem.ls)

    def dma(q, out, in_, r=(), w=(), ext=(), sem=None):
        e = {"y": Y, "a": S}[q]
        op(q, lambda: e.dma_start(out, in_), r, w, ext, True, sem)

    def ts(out, in0, s1, s2, o0, o1=None, r=(), w=()):
        if o1 is None:
            op("v", lambda: V.tensor_scalar(out, in0, s1, None, o0), r, w)
        else:
            op("v", lambda: V.tensor_scalar(out, in0, s1, s2, o0, o1), r, w)

    def tt(out, a, b, o, r=(), w=()):
        op("v", lambda: V.tensor_tensor(out, a, b, o), r, w)

    def cp(out, a, r=(), w=()):
        op("v", lambda: V.tensor_copy(out, a), r, w)

    def fill(out, c, w=()):
        op("v", lambda: V.memset(out, c), (), w)

    def act(out, a, r=(), w=()):
        op("a", lambda: S.activation(out, a, F.Copy), r, w)

    def mm(out, l, rh, st, sp, r=(), w=()):
        op("p", lambda: P.matmul(out, l, rh, st, sp), r, w)

    def iota(out, pat, w):
        op("g", lambda: g.iota(out, pat, 0, 0, allow_small_or_imprecise_dtypes=True), (), w)

    if me == 0:
        dma("y", T.pk0[:, 0:64, :], T.kids[:], w=["send+"])
        dma("a", T.pk0[:, 64:96, :], T.runs[:], w=["send+"])
        dma("y", T.pk0[:, 96:128, :], T.letter[:], w=["send+"])
    else:
        dma("y", T.sendK[:], T.kids[:], w=["send"])
    dma("a", T.sendQ[:, 0:64, :], T.top[:], w=["sendQ+"])
    dma("a" if me else "y", T.sendQ[:, 64:128, :], T.off[:], w=["sendQ+"])
    if me:
        dma("y", T.landK[me], T.kids[me:me + 1, :], sem="arrK%d" % me)
    dma("y", T.landQ[me, 0:64, :], T.top[16 * me:16 * me + 16, :], sem="arrQ")
    dma("y", T.landQ[me, 64:128, :], T.off[16 * me:16 * me + 16, :], sem="arrQ")

    def arr(h):
        if h == me:
            return [] if h == 0 else [("arrK%d" % h, 16)]
        return [("arrK%d" % h, 1)]

    def first(a, b):
        return T.pk0[0, a:b, :] if me == 0 else T.land0[a:b, :]
    own0 = ["send"] if me == 0 else []

    op("g", lambda: g.iota(T.PI[:, 0:1], [[0, 1]], 0, 1), (), ["PI0"])
    iota(T.J16[:], [[0, 8], [1, 16]], ["J16"])
    iota(T.J8[:], [[0, 16], [1, 8]], ["J8"])
    iota(T.J128[:], [[1, 128]], ["J128"])

    if me == 0:
        op("g", lambda: spread(lambda r: T.pk0[r], T.land0[:], "arrK0"), r=["send"])
    else:
        op("g", lambda: spread(lambda r: T.sendK[r], T.landK[me], "arrK%d" % me), r=["send"])
    op("g", lambda: spread(lambda r: T.sendQ[r], T.landQ[me], "arrQ"), r=["sendQ"])

    fill(T.X[:, 0:1024], 0.0, ["X0"])
    fill(T.CT[:], 0, ["CT"])
    fill(T.RS[:], 0.0, ["RS0"])
    fill(T.RF[:], 0.0, ["RF0"])
    fill(T.RB[:], 0.0, ["RB0"])
    fill(T.O4[:], 0.0, ["O40"])
    fill(T.tb[:, 0:16], 1.0, ["tb"])
    act(T.CO[:], T.X[:, 0:640], ["X0"], ["COz"])
    act(T.X[:, 1024:2048], T.X[:, 0:1024], ["X0"], ["XA+"])
    act(T.X[:, 2048:3072], T.X[:, 0:1024], ["X0"], ["XB+"])
    act(T.X[:, 3072:4096], T.X[:, 0:1024], ["X0"], ["XB+"])
    pi = T.PI[:, 0:1]
    ts(T.PB[:, 0:1], pi, 15, None, A.bitwise_and, r=["PI0"], w=["PB+"])
    ts(T.PB[:, 1:2], pi, 7, None, A.bitwise_and, r=["PI0"], w=["PB+"])
    ts(T.PB[:, 2:3], pi, 4, None, A.logical_shift_right, r=["PI0"], w=["PB+"])
    ts(T.PB[:, 3:4], pi, 4, 1, A.logical_shift_right, A.bitwise_and, r=["PI0"], w=["PB+"])
    ts(T.PB[:, 4:5], pi, 5, None, A.logical_shift_right, r=["PI0"], w=["PB+"])
    ts(T.PB[:, 5:6], pi, 3, 1, A.logical_shift_right, A.bitwise_and, r=["PI0"], w=["PB+"])
    cp(T.PF[:, 6:7], pi, ["PI0"], ["PF+"])
    cp(T.PF[:, 0:6], T.PB[:, 0:6], ["PB"], ["PF+"])
    p16, p8, grp, g1, g2, hi, pf = [T.PF[:, k:k + 1] for k in range(7)]
    pa = [T.PA[:, k:k + 1] for k in range(32)]
    ts(pa[0], g1, 4.0, g2, A.mult, A.add, ["PF"], ["c+"])
    ts(pa[1], hi, -100.0, None, A.mult, None, ["PF"], ["c+"])
    ts(pa[2], hi, 100.0, -100.0, A.mult, A.add, ["PF"], ["c+"])
    ts(pa[6], hi, -1.0, None, A.add, None, ["PF"], ["c+"])
    ts(pa[7], hi, -1.0, None, A.mult, None, ["PF"], ["c+"])
    ts(pa[8], hi, 2.0, -1.0, A.mult, A.add, ["PF"], ["c+"])
    ts(pa[15], hi, 1.0 / 512 - 1.0, 1.0, A.mult, A.add, ["PF"], ["c+"])
    D, D32, I = T.LH[:, 0:128], T.LF[:, 0:128], T.LH[:, 896:1024]
    ts(D, T.J16[:], p16, None, A.is_equal, None, ["J16", "PF"], ["D"])
    ts(T.MK[:], T.J8[:, 0:8], p8, None, A.is_equal, None, ["J8", "PF"], ["MK"])
    ts(D32, T.J16[:], p16, None, A.is_equal, None, ["J16", "PF"], ["D32"])
    ts(pa[3], pa[0], pa[1], None, A.add, None, ["c"], ["a+"])
    ts(pa[4], pa[0], 2.0, pa[1], A.mult, A.add, ["c"], ["a+"])
    ts(pa[5], pa[0], 2.0, pa[2], A.mult, A.add, ["c"], ["a+"])
    ts(pa[9], pa[6], p8, 1048576.0, A.mult, A.mult, ["c", "PF"], ["a+"])
    ts(pa[10], pa[6], p8, -1048576.0, A.mult, A.mult, ["c", "PF"], ["a+"])
    E = T.LF
    ts(T.PA[:, 12:15], E[:, 0:3], 4096.0, None, A.mult, None, ["D32"], ["k+"])
    tt(T.PA[:, 16:19], E[:, 4:10:2], E[:, 5:10:2], A.add, ["D32"], ["k+"])
    ts(T.PA[:, 20:23], E[:, 5:10:2], -1.0, None, A.mult, None, ["D32"], ["k+"])
    ts(pa[11], E[:, 0:1], -4096.0, None, A.mult, None, ["D32"], ["k+"])
    LS = [T.LH[:, 128:256], T.LH[:, 256:384]]
    LC = [T.LH[:, 384:512], T.LH[:, 512:640]]
    LO = [T.LH[:, 640:768], T.LH[:, 768:896]]
    LC32 = [T.LF[:, 128:256], T.LF[:, 256:384]]
    ts(LS[0], T.J8[:], pa[3], None, A.is_equal, None, ["J8", "a"], ["LS+"])
    ts(LS[1], T.J16[:], pa[3], None, A.is_equal, None, ["J16", "a"], ["LS+"])
    tt(T.PA[:, 24:27], T.PA[:, 12:15], T.PA[:, 16:19], A.subtract, ["k"], ["kk+"])
    ts(T.PA[:, 28:31], T.PA[:, 16:19], -1.0, None, A.mult, None, ["k"], ["kk+"])
    for t in range(2):
        ts(LC[t], T.J16[:], -float(t), pa[5], A.add, A.is_equal, ["J16", "a"], ["LC+"])
        ts(LO[t], T.J16[:], -float(t), pa[4], A.add, A.is_equal, ["J16", "a"], ["LC+"])
        ts(LC32[t], T.J16[:], -float(t), pa[5], A.add, A.is_equal, ["J16", "a"], ["LC+"])
    cp(T.OC[:], T.J8[:, 0:8], ["J8"], ["OC"])
    ts(I, T.J128[:], pf, None, A.is_equal, None, ["J128", "PF"], ["I"])
    ts(T.CW[:], T.J128[:], 2.0, 1.0, A.mult, A.add, ["J128"], ["CW"])

    for key, c, n, coef in (("RF", 0, 8, 1.0), ("RF", 112, 1, E[:, 13:14]), ("RF", 120, 1, E[:, 3:4]),
                            ("RB", 0, 1, pa[10]), ("RB", 16, 1, pa[9]), ("RB", 24, 1, pa[12]), ("RB", 40, 1, pa[11]),
                            ("RS", 104, 2, 1.0), ("RS", 128, 6, pa[6]), ("RS", 176, 1, pa[7]), ("RS", 192, 1, pa[8]),
                            ("RS", 200, 1, pa[6]), ("RS", 0, 1, pa[24]),
                            ("RS", 24, 1, pa[25]), ("RS", 32, 1, pa[29]), ("RS", 40, 1, E[:, 6:7]), ("RS", 72, 2, pa[21]),
                            ("RS", 48, 1, pa[26]), ("RS", 56, 1, pa[30]), ("RS", 64, 1, E[:, 8:9]), ("RS", 88, 2, pa[22])):
        ts(T[key][:, c:c + 8 * n], T.J8[:, 0:8 * n], grp, coef, A.is_equal, A.mult,
           ["J8", "PF", "c", "a", "k", "kk", "D32", key + "0"], [key + "+"])

    lo_op = len(ops)

    def zload(q, h, b):
        src = first(32 * b, 32 * b + 32) if h == 0 else T.landK[h, 64 * b:64 * b + 64, :]
        c = 32 * (h // 2) + 16 * b
        dma(q, T.Z[h % 2::2, c:c + 16], src, own0 if h == 0 else [], ["Z%d+" % min(h // 2, 1)], arr(h))
    zload("y", 1, 0)
    zload("a", 1, 1)
    dma("y", T.CT[16:128, :], T.landK[1:8], ["CT"], ["CT1"], [x for h in range(1, N) for x in arr(h)])
    dma("y", T.RU[0:16, :], first(64, 128), own0, ["RU"], arr(0))
    zload("a", 0, 1)
    zload("y", 0, 0)
    for h in range(2, TOP + 1):
        zload("y", h, 0)
        zload("y", h, 1)
    dma("y", T.topP[:], T.landQ[:, 0:64, :], w=["topP"], ext=[("arrQ", 32 + N - 1)])
    dma("y", T.offP[:], T.landQ[:, 64:128, :], w=["offP"], ext=[("arrQ", 32 + N - 1)])

    pos = {0: 0, 1: 1, 2: 2, 4: 3, 3: 4, 5: 5}
    C1, C2 = 1.0 / 128, -0.5 + 1.0 / 256

    def turn(a, b, k):
        cp(T.Zf[:, a:b], T.Z[:, a:b], ["Z%d" % k], ["Zf%d" % k])
        op("v", lambda: V.transpose(T.Zt[:, a:b], T.Zf[:, a:b]), ["Zf%d" % k], ["Zt%d" % k])

    def low(a, b, k):
        cp(T.Zi[:, a:b], T.Zt[:, a:b], ["Zt%d" % k], ["Zi%d" % k])

    def low2(a, b, k):
        ts(T.Za[:, a:b], T.Zi[:, a:b], 127, None, A.bitwise_and, None, ["Zi%d" % k], ["Za%d" % k])

    def classes(c, a, b, k, hs):
        n = len(range(a, b, 2))
        ts(T.cls[:, c:c + n], T.Zt[:, a:b:2], C1, C2, A.mult, A.add, ["Zt%d" % k], ["cls%d" % h for h in hs])

    def columns(c, a, b, k, hs):
        n = len(range(a, b, 2))
        cp(T.col[:, c:c + n], T.Za[:, a:b:2], ["Za%d" % k], ["col%d" % h for h in hs])

    def mask(h, t0, t1):
        c = 16 * pos[h]
        act(T.M[:, 256 * h + 128 * t0:256 * h + 128 * t1], T.MK[:, 0:8].indirect(T.cls[:, c + 8 * t0:c + 8 * t1]),
            ["MK", "cls%d" % h], ["M%d" % (2 * h + t) for t in range(t0, t1)])

    def pick(out, win, offs, m, r, w):
        tt(out, win.indirect(offs), T.M[:, 128 * m:128 * m + 128], A.mult, list(r) + ["M%d" % m], w)

    def cbank(h):
        if h == TOP:
            return T.pD0, "P:D0", 0
        return (T.pC0, "P:C0", 96 * (h - 2)) if h % 2 == 0 else (T.pC1, "P:C1", 96 * (h - 1))

    def compact_l(h, t):
        pc, key, o = cbank(h)
        c = 256 * h + 128 * t
        mm(pc[:, o:o + 128], LC[t], T.G[:, c:c + 128], t == 0, t == 1, ["LC", "G%d" % (2 * h + t)], [key])

    def obank(h):
        return (T.pD1, "P:D1", 0) if h == TOP else cbank(h)

    def compact_o(h):
        pc, key, o = obank(h)
        for t in range(2):
            c = 256 * h + 128 * t
            mm(pc[:, o + 128:o + 192], LO[t], T.G[:, c:c + 128:2], t == 0, t == 1, ["LC", "G%d" % (2 * h + t)], [key])

    def compact(h):
        compact_l(h, 0)
        compact_l(h, 1)
        compact_o(h)

    def narrow_l(h):
        pc, key, o = cbank(h)
        c = 128 * (h - 1)
        act(T.CL[:, c:c + 128], pc[:, o:o + 128], [key], ["CL%d" % h])

    def narrow_o(h):
        pc, key, o = obank(h)
        c = 128 * (h - 1)
        act(T.CO[:, c + 1:c + 128:2], pc[:, o + 128:o + 192], [key, "COz"], ["CO%d" % h])

    def narrow(h):
        narrow_l(h)
        narrow_o(h)

    def widen(h, which=(0, 1)):
        c, w, f, xk = 128 * (h - 1), 2048 * (h % 2), h // 2, "XB" if h % 2 else "XA"
        if 0 in which:
            dma("y", T.X[4 + 2 * f::16, w:w + 2048], T.CL[:, c:c + 128], ["CL%d" % h, "Xc"], [xk + "+"])
        if 1 in which:
            dma("y", T.X[5 + 2 * f::16, w:w + 2048], T.CO[:, c:c + 128], ["CO%d" % h, "Xc"], [xk + "+"])

    def kids_rows():
        ts(T.CF[:], T.CT[:], 2.0, 1.0, A.mult, A.add, ["CT", "CT1"], ["CF"])
        for k in range(8):
            dma("y", T.X[16 * k:16 * k + 4, 0:4096], T.CF[:], ["CF", "X0", "XA", "XB", "COz"], ["Xc+"])
            dma("y", T.X[16 * k + 13:16 * k + 14, 1:4097], T.CF[96:128, :], ["CF", "X0", "XA", "XB", "COz"], ["Xc+"])

    def letters_c(t):
        pick(T.GL[:, 128 * t:128 * t + 128], T.WW[:, 0:128], T.col[:, 8 * t:8 * t + 8], t, ["W0", "col0"], ["GL%d" % t])

    def letters_d(u):
        for t in range(2):
            c = 128 * t + 64 * u
            mm(T.pL[:, 64 * u:64 + 64 * u], LC32[t], T.GL[:, c:c + 64], t == 0, t == 1, ["LC", "GL%d" % t], ["P:L"])

    def letters_e():
        act(T.CL[:, 640:768], T.pL[:, 0:128], ["P:L"], ["CLet"])

    def letters_f():
        dma("y", T.X[12::16, 0:2048], T.CL[:, 640:768], ["CLet", "Xc"], ["XA+"])

    RE = T.RF[:, 112:128]

    def open_a():
        ts(T.e1[:, 0:8], T.topP[:], 2.0, 1.0, A.mult, A.add, ["topP"], ["e1"])

    def open_b():
        act(T.GE[:, 0:128], T.X[:, 2048:4096].indirect(T.e1[:, 0:8]), ["e1", "Xc", "XB"], ["GE1"])

    def open_c():
        mm(T.pD1[:, 0:16], T.GE[:, 0:128], RE, True, True, ["GE1", "RF"], ["P:D1"])

    def open_d():
        cp(T.e1[:, 8:24], T.pD1[:, 0:16], ["P:D1"], ["e2"])
        act(T.GE[:, 128:384], T.X[:, 0:2048].indirect(T.e1[:, 8:24]), ["e2", "Xc", "XA", "X0"], ["GE2"])

    def open_e():
        for b in range(2):
            mm(T.pD1[:, 16 + 16 * b:32 + 16 * b], T.GE[:, 128 + 128 * b:256 + 128 * b], RE, True, True, ["GE2", "RF"], ["P:D1"])

    def open_f():
        ts(T.tu[:, 0:32], T.pD1[:, 16:48], 1.0 / 256, -0.5, A.mult, A.add, ["P:D1"], ["tcls"])
        ts(T.ti[:, 0:32], T.pD1[:, 16:48], 0.5, -0.5, A.mult, A.add, ["P:D1"], ["ti"])

    def open_m(u):
        act(T.M[:, 1536 + 256 * u:1792 + 256 * u], T.MK[:, 0:8].indirect(T.tu[:, 16 * u:16 * u + 16]), ["MK", "tcls"],
            ["M%d" % (12 + 2 * u), "M%d" % (13 + 2 * u)])

    def open_g():
        ts(T.ti[:, 32:64], T.ti[:, 0:32], 127, None, A.bitwise_and, None, ["ti"], ["ta"])

    def open_h():
        cp(T.tu[:, 32:64], T.ti[:, 32:64], ["ta"], ["tcol"])

    def open_n(u):
        act(T.GN[:, 256 * u:256 * u + 256], T.CW[:, 0:128].indirect(T.tu[:, 32 + 16 * u:48 + 16 * u]), ["CW", "tcol"], ["GN%d" % u])

    def places_a():
        tt(T.GO[:], T.offP[:, 0:8].indirect(T.OC[:, 0:8]), D32, A.mult, ["offP", "OC", "D32"], ["GO32"])

    def places_b():
        mm(T.pT[:, 0:112], T.GO[:], T.RF[:, 0:112], True, False, ["GO32", "RF"], ["P:T"])

    def names(k, which):
        c, n = 48 + 16 * k, 24 if k < 3 else 8
        if which == 0:
            mm(T.pT[:, c:c + n], T.M[:, 1536 + 128 * k:1664 + 128 * k], T.RB[:, 0:n], False, False, ["M%d" % (12 + k), "RB"], ["P:T"])
        else:
            mm(T.pT[:, c:c + n], T.GN[:, 128 * k:128 * k + 128], T.RB[:, 24:24 + n], False, False, ["GN%d" % (k // 2), "RB"], ["P:T"])

    ts(T.RUf[0:16, :], T.RU[0:16, :], T.PA[0:16, 15:16], None, A.mult, None, ["RU", "c"], ["RUf"])
    mm(T.pW[:, 0:128], T.LF[0:16, 0:128], T.RUf[0:16, :], True, True, ["D32", "RUf"], ["P:W"])
    kids_rows()
    cp(T.Zf[:, 0:32], T.Z[:, 0:32], ["Z0"], ["Zf0"])
    ts(T.Za[:, 0:32], T.Z[:, 0:32], 127, None, A.bitwise_and, None, ["Z0"], ["Za0"])
    op("v", lambda: V.transpose(T.Zt[:, 0:32], T.Zf[:, 0:32]), ["Zf0"], ["Zt0"])
    cp(T.Zl[:, 0:32], T.Za[:, 0:32], ["Za0"], ["Zl0"])
    classes(0, 0, 32, 0, [0])
    op("v", lambda: V.transpose(T.Zl[:, 32:64], T.Zl[:, 0:32]), ["Zl0"], ["Zl1"])
    mask(0, 0, 1)
    mask(0, 1, 2)
    cp(T.WW[:, 0:128], T.pW[:, 0:128], ["P:W"], ["W0"])
    cp(T.col[:, 0:16], T.Zl[:, 32:64:2], ["Zl1"], ["col0"])
    classes(16, 1, 32, 0, [1])
    mask(1, 0, 2)

    L = lambda fn, *a: (lambda: fn(*a))
    mid = {
        0: [L(cp, T.col[:, 16:32], T.Zl[:, 33:64:2], ["Zl1"], ["col1"]), L(turn, 32, 96, 1), L(classes, 32, 32, 96, 1, [2, 4]),
            L(classes, 64, 33, 96, 1, [3, 5]), L(low, 32, 96, 1), L(mask, 2, 0, 2), L(mask, 3, 0, 2), L(mask, 4, 0, 2)],
        1: [L(low2, 32, 96, 1), open_a, L(columns, 32, 32, 96, 1, [2, 4]), L(letters_c, 0), L(compact, 1), L(narrow, 1), open_b],
        2: [L(letters_c, 1), open_c, L(compact, 2), L(columns, 64, 33, 96, 1, [3, 5]), L(widen, 1), L(mask, 5, 0, 2), open_d],
        3: [places_a, open_e, L(letters_d, 0), L(letters_d, 1), letters_e, L(narrow, 2), letters_f, L(widen, 2)],
        4: [open_g, L(compact, 3), places_b, open_h, L(narrow, 3), L(widen, 3), L(open_n, 0)],
        5: [L(compact_o, 5), L(narrow_o, 5), L(widen, 5, (1,)), L(compact, 4), L(open_n, 1), L(narrow, 4), L(widen, 4)],
    }
    end = {3: [open_f, L(open_m, 0), L(open_m, 1)]}

    for h in range(TOP + 1):
        c0 = 16 * pos[h]
        for t in range(2):
            c = 256 * h + 128 * t
            pick(T.G[:, c:c + 128], T.WW[:, 128 * h:128 * h + 128], T.col[:, c0 + 8 * t:c0 + 8 * t + 8], 2 * h + t,
                 ["W%d" % h, "col%d" % h], ["G%d" % (2 * h + t)])
            if h == TOP:
                compact_l(h, t)
                if t:
                    narrow_l(h)
                    widen(h, (0,))
            for b in range(2):
                mm((T.pW, T.pV)[t][:, 0:64], LS[b], T.G[:, c + b:c + 128:2], b == 0, b == 1, ["LS", "G%d" % (2 * h + t)], [("P:W", "P:V")[t]])
        for fn in mid[h]:
            fn()
        cp(T.WW[:, 128 * h + 128:128 * h + 192], T.pW[:, 0:64], ["P:W"], ["W%d+" % (h + 1)])
        cp(T.WW[:, 128 * h + 192:128 * h + 256], T.pV[:, 0:64], ["P:V"], ["W%d+" % (h + 1)])
        for fn in end.get(h, []):
            fn()

    for k in range(4):
        gt = T.G[:, 1536 + 128 * k:1664 + 128 * k]
        pick(gt, T.WW[:, 768:896], T.tu[:, 32 + 8 * k:40 + 8 * k], 12 + k, ["W6", "tcol"], ["GT%d" % k])
        if k == 0:
            for kk in range(4):
                names(kk, 0)
            names(0, 1)
            names(1, 1)
        if k == 2:
            names(2, 1)
            names(3, 1)
        if k < 3:
            mm(T.pT[:, 16 * k:48], gt, T.RS[:, 128:176 - 16 * k], False, False, ["GT%d" % k, "RS"], ["P:T"])
        c, n = 48 + 16 * k, 32 if k < 3 else 8
        mm(T.pT[:, c:c + n], gt, T.RS[:, 176:176 + n], False, k == 3, ["GT%d" % k, "RS"], ["P:T"])
    I1, I2 = 1.0 / 4096, -0.5 + 1.0 / 8192
    ts(T.tb[:, 16:64], T.pT[:, 0:48], 0.0, None, A.is_ge, None, ["P:T", "tb"], ["tb0"])
    tt(T.tb[:, 64:128], T.tb[:, 0:64], T.pT[:, 48:112], A.mult, ["tb0", "P:T"], ["tb1"])
    tt(T.tb[:, 128:160], T.tb[:, 64:96], T.tb[:, 96:128], A.add, ["tb1"], ["tb2"])
    tt(T.YU[:], T.tb[:, 128:144], T.tb[:, 144:160], A.add, ["tb2"], ["YU"])
    ts(T.ix[:, 40:48], T.YU[:, 0:8], I1, I2, A.mult, A.add, ["YU"], ["ix5"])
    GO = T.GD[:, 0:128]
    tt(GO, T.YU[:, 8:16].indirect(T.OC[:, 0:8]), D, A.mult, ["YU", "OC", "D"], ["GO"])
    ts(T.RM[:], T.YU[:, 0:8], 4095, None, A.bitwise_and, None, ["YU"], ["RM"])

    bank = {5: (T.pD1, "P:D1"), 4: (T.pD0, "P:D0"), 3: (T.pC0, "P:C0"), 2: (T.pC1, "P:C1"), 1: (T.pW, "P:W")}

    def settle():
        for k in range(2):
            tt(T.O4[:, 8 * k:8 * k + 8], T.RM[:], T.YU[:, 8:16], A.min, ["RM", "YU", "O40"], ["O4+"])
    todo = [settle]
    for h in range(TOP, 0, -1):
        w, xk = 2048 * (h % 2), "XB" if h % 2 else "XA"
        pd, key = bank[h]
        n = 24 if h >= 3 else 8
        m = min(n, 16)
        if h % 2:
            mm(pd[:, 0:n], GO, T.RS[:, 104:104 + n], True, False, ["GO", "RS"], [key])
        else:
            mm(pd[:, 0:n], I, T.O4[:, 0:n], True, False, ["I", "O4"], [key])
        for e in range(h + 2, TOP + 1, 2):
            c = 56 + 16 * (e // 2)
            mm(pd[:, 0:m], T.GD[:, 128 * e:128 * e + 128], T.RS[:, c:c + m], False, False, ["GD%d" % e, "RS"], [key])
        for e in range(TOP if h % 2 else TOP - 1, h, -2):
            for c in range(0, m, 8):
                mm(pd[:, c:c + 8], I, T.TT[:, 8 * e:8 * e + 8], False, False, ["I", "TT%d" % e], [key])
        gd = T.GD[:, 128 * h:128 * h + 128]
        cp(gd, T.X[:, w:w + 2048].indirect(T.ix[:, 8 * h:8 * h + 8]), ["ix%d" % h, "Xc", xk, "X0"], ["GD%d" % h])
        mm(pd[:, 0:n], gd, T.RS[:, 24 * (h // 2):24 * (h // 2) + n], False, True, ["GD%d" % h, "RS"], [key])
        for fn in todo:
            fn()
        todo = []
        ts(T.ix[:, 8 * h - 8:8 * h], pd[:, 0:8], I1, I2, A.mult, A.add, [key], ["ix%d" % (h - 1)])
        if h >= 3:
            def after(h=h, pd=pd, key=key):
                ts(T.B[:, 8 * h:8 * h + 8], pd[:, 8:16], 0.0, -1.0, A.is_ge, A.mult, [key], ["B%d" % h])
                tt(T.TT[:, 8 * h:8 * h + 8], T.B[:, 8 * h:8 * h + 8], pd[:, 16:24], A.mult, ["B%d" % h, key], ["TT%d" % h])
            todo.append(after)
    op("a", lambda: S.activation(T.GF[:, 64:128], T.X[:, 0:2048].indirect(T.ix[:, 4:8]), F.Copy, scale=512.0), ["ix0", "Xc", "XA", "X0"], ["GF+"])
    ts(T.GF[:, 0:64], T.X[:, 0:2048].indirect(T.ix[:, 0:4]), 512.0, None, A.mult, None, ["ix0", "Xc", "XA", "X0"], ["GF+"])

    hi_op = len(ops)
    dma("y", T.outD[:], T.GF[12::16, :], ["GF"], ["outD"])
    dma("a", T.landY[me], T.GF[16 * me + 12:16 * me + 13, :], ["GF"], sem="arrY")
    op("g", lambda: spread(lambda r: T.outD[r], T.landY[me], "arrY"), r=["outD"])
    dma("y", T.y[:], T.landY[:], ext=[("arrY", 16 + N - 1)])

    order = list(range(lo_op)) + [lo_op + k for k in (ORDER or range(hi_op - lo_op))] + list(range(hi_op, len(ops)))
    emit(ops, order, {"v": V, "a": S, "p": P, "y": Y, "g": g}, T)
    g.wait_ge(T.sem.ls, sent[0])
